import numpy as np
import ml_dtypes

BF16 = ml_dtypes.bfloat16


def bf(x):
    return np.asarray(x, np.float32).astype(BF16)


def f32(x):
    return np.asarray(x, np.float32)


def f64(x):
    return np.asarray(x).astype(np.float64)


def striped(idx):
    return np.tile(idx.reshape(-1, 16).T, (8, 1))


S, K, M, N, E, Q = 1024, 128, 512, 2048, 4, 512


def sigmoid(v):
    return 1.0 / (1.0 + np.exp(-v))


def two_experts():
    first = np.random.permutation(S).reshape(E, S // E)
    return np.concatenate([np.random.permutation(np.concatenate([first[e], first[(e + 1) % E]])) for e in range(E)])


def setup_inputs():
    return {"table": bf(np.random.standard_normal((K, S))), "w": bf(np.random.standard_normal((E, K, M)) / np.sqrt(K)), "b": f32(0.5 * np.random.standard_normal((M, 1))), "offs": striped(two_experts())}


def reference(table, w, b, offs):
    idx = offs[:16].T.reshape(-1)
    x = f64(table)[:, idx]
    y = np.concatenate([f64(w)[e].T @ x[:, e * Q : (e + 1) * Q] for e in range(E)], axis=1)
    return (y + f64(b)) * sigmoid(y + f64(b))

import concourse.mybir as mybir

P = 128
S = 1024
M = 512
E = 4
Q = 512
N = E * Q
LANES = 16

FLOPS = 2 * P * M * N

BF16, F32, U16 = mybir.dt.bfloat16, mybir.dt.float32, mybir.dt.uint16
SILU = mybir.ActivationFunctionType.Silu


def tile_gather_matmul_kernel(tc, table, w, b, offs, out):
    nc = tc.nc
    blocks = M // P
    k = Q // LANES
    with (
        tc.tile_pool(name="held", bufs=1) as held,
        tc.tile_pool(name="results", bufs=E * blocks) as results,
        tc.psum_pool(name="banks", bufs=8) as banks,
    ):
        tokens = held.tile([P, S], BF16, name="tokens")
        offsets = held.tile([P, N // LANES], U16, name="offsets")
        weights = [held.tile([P, M], BF16, name=f"weights{e}") for e in range(E)]
        bias = held.tile([P, blocks], F32, name="bias")
        warm = held.tile([P, 1], F32, name="warm")

        nc.sync.dma_start(tokens[:], table)
        nc.scalar.dma_start(weights[0][:], w[0])
        nc.sync.dma_start(offsets[:], offs)
        nc.scalar.dma_start(bias[:], b.rearrange("(a p) o -> p (a o)", p=P))
        for e in range(1, E):
            nc.sync.dma_start(weights[e][:], w[e])

        nc.vector.memset(warm[:], 0.0)
        nc.scalar.activation(warm[:], warm[:], SILU)

        for e in range(E):
            piece = offsets[:, e * k : (e + 1) * k]
            for a in range(blocks):
                y = banks.tile([P, Q], F32, name="y")
                nc.tensor.matmul(y[:], weights[e][:, a * P : (a + 1) * P], tokens[:].indirect(piece), start=True, stop=True)
                result = results.tile([P, Q], F32, name="result")
                nc.scalar.activation(result[:], y[:], SILU, bias=bias[:, a : a + 1])
                nc.sync.dma_start(out[a * P : (a + 1) * P, e * Q : (e + 1) * Q], result[:])
